import numpy as np, ml_dtypes
CORES = [22,38,54,62,70,110,23,39,55,63,71,111]
N = 12
W, KW, DIL = 512, 3, 16
H = (KW // 2) * DIL
def setup_inputs(rng):
    return {"x": rng.standard_normal((N, 128, W), dtype=np.float32).astype(ml_dtypes.bfloat16), "w": rng.standard_normal((N, 128, KW * 128), dtype=np.float32).astype(ml_dtypes.bfloat16)}
def setup_inputs_big(rng):
    d = setup_inputs(rng)
    for k in ("x", "w"): d[k] = (d[k].astype(np.float32) * 1024.0).astype(d[k].dtype)
    return d
def setup_inputs_small(rng):
    d = setup_inputs(rng)
    for k in ("x", "w"): d[k] = (d[k].astype(np.float32) * (1 / 1024.0)).astype(d[k].dtype)
    return d
def reference(x, w):
    X, W_ = x.astype(np.float64), w.astype(np.float64)
    g = np.concatenate(list(X), axis=1)
    p = np.concatenate([g[:, -H:], g, g[:, :H]], axis=1)
    y = np.zeros((N, 128, W))
    for r in range(N):
        for i in range(KW):
            y[r] += W_[r][:, 128 * i:128 * i + 128].T @ p[:, W * r + i * DIL:W * r + i * DIL + W]
    return {"y": y.astype(ml_dtypes.bfloat16 if x.dtype != np.float64 else np.float64)}

from concourse.bass import DstId, RemoteDMATransfer

WID, HALO, TAPS, CH = 512, 16, 3, 128
ENGINES = 4

SCRATCH = {
    "xe": ("sbuf", [CH, WID + 2 * HALO], "bfloat16"),
    "ws": ("sbuf", [CH, TAPS * CH], "bfloat16"),
    "ys": ("sbuf", [CH, WID], "bfloat16"),
    "pi": ("psum", [CH, 512], "float32"),
    "pl": ("psum", [CH, 512], "float32"),
    "pr": ("psum", [CH, 512], "float32"),
}
SEMAPHORES = ["edge", "main", "sent", "hl", "hr", "mi", "ml", "mr", "ci", "cl", "cr", "done"]


def _hops(topo, a, b):
    ca, cb = topo.chip(a), topo.chip(b)
    if ca == cb:
        return 0
    return 1 if (topo.mates(ca, cb) or topo.same_plane(ca, cb)) else 2


def rank_program(g, core, T, topo):
    rank = T.rank_of(core)
    if rank is None:
        return
    n = len(T.cores)
    left, right = T.cores[(rank - 1) % n], T.cores[(rank + 1) % n]
    assert topo.may_write(core, left) and topo.may_write(core, right)
    S = T.sem
    xe, ws, ys = T.xe, T.ws, T.ys
    lo, hi = HALO, HALO + WID

    g.sync.dma_start(xe[:, lo:lo + HALO], T.x[:, 0:HALO]).then_inc(S.edge, 16)
    g.scalar.dma_start(xe[:, hi - HALO:hi], T.x[:, WID - HALO:WID]).then_inc(S.edge, 16)
    g.sync.dma_start(xe[:, lo + HALO:hi - HALO], T.x[:, HALO:WID - HALO]).then_inc(S.main, 16)
    g.scalar.dma_start(ws[:], T.w[:]).then_inc(S.main, 16)

    both = topo.mask(core, left) & topo.mask(core, right)
    bits = [1 << b for b in range(16) if (both >> b) & 1]
    m_l, m_r = sum(bits[0:ENGINES]), sum(bits[ENGINES:2 * ENGINES])
    rid_l, pid_l, _ = topo.addr(left)
    rid_r, pid_r, _ = topo.addr(right)
    g.wait_ge(S.edge, 32)
    g.remote_dma_fused(
        [
            RemoteDMATransfer(dst_ids=[DstId(rid=rid_l, pnc=pid_l)], dma_engine_mask=m_l, remote_sem=S.hr,
                              src=xe[:, lo:lo + HALO], dst=xe[:, hi:hi + HALO]),
            RemoteDMATransfer(dst_ids=[DstId(rid=rid_r, pnc=pid_r)], dma_engine_mask=m_r, remote_sem=S.hl,
                              src=xe[:, hi - HALO:hi], dst=xe[:, 0:HALO]),
        ],
        local_sem=S.sent,
    )

    def tap(i):
        return ws[:, CH * i:CH * (i + 1)]

    t = g.tensor
    t.wait_ge(S.edge, 32)
    t.wait_ge(S.main, 32)
    inner = WID - 2 * HALO
    for i in range(TAPS):
        t.matmul(T.pi[:, 0:inner], tap(i), xe[:, HALO + HALO * i:HALO + HALO * i + inner],
                 start=(i == 0), stop=(i == TAPS - 1)).then_inc(S.mi, 1)
    t.matmul(T.pl[:, 0:HALO], tap(1), xe[:, HALO:2 * HALO], start=True, stop=False).then_inc(S.ml, 1)
    t.matmul(T.pl[:, 0:HALO], tap(2), xe[:, 2 * HALO:3 * HALO], start=False, stop=False).then_inc(S.ml, 1)
    b = WID - HALO
    t.matmul(T.pr[:, 0:HALO], tap(0), xe[:, b:b + HALO], start=True, stop=False).then_inc(S.mr, 1)
    t.matmul(T.pr[:, 0:HALO], tap(1), xe[:, b + HALO:b + 2 * HALO], start=False, stop=False).then_inc(S.mr, 1)

    sides = ["l", "r"] if _hops(topo, left, core) <= _hops(topo, right, core) else ["r", "l"]
    for s in sides:
        if s == "l":
            t.wait_ge(S.hl, ENGINES)
            t.matmul(T.pl[:, 0:HALO], tap(0), xe[:, 0:HALO], start=False, stop=True).then_inc(S.ml, 1)
        else:
            t.wait_ge(S.hr, ENGINES)
            t.matmul(T.pr[:, 0:HALO], tap(2), xe[:, hi:hi + HALO], start=False, stop=True).then_inc(S.mr, 1)

    v = g.vector
    v.wait_ge(S.mi, TAPS)
    v.tensor_copy(ys[:, HALO:WID - HALO], T.pi[:, 0:inner]).then_inc(S.ci, 1)
    for s in sides:
        if s == "l":
            v.wait_ge(S.ml, TAPS)
            v.tensor_copy(ys[:, 0:HALO], T.pl[:, 0:HALO]).then_inc(S.cl, 1)
        else:
            v.wait_ge(S.mr, TAPS)
            v.tensor_copy(ys[:, WID - HALO:WID], T.pr[:, 0:HALO]).then_inc(S.cr, 1)

    g.sync.wait_ge(S.ci, 1)
    g.sync.dma_start(T.y[:, HALO:WID - HALO], ys[:, HALO:WID - HALO]).then_inc(S.done, 16)
    g.sync.wait_ge(S.cl, 1)
    g.sync.dma_start(T.y[:, 0:HALO], ys[:, 0:HALO]).then_inc(S.done, 16)
    g.scalar.wait_ge(S.cr, 1)
    g.scalar.dma_start(T.y[:, WID - HALO:WID], ys[:, WID - HALO:WID]).then_inc(S.done, 16)

    g.wait_ge(S.sent, 2 * ENGINES)
    g.wait_ge(S.done, 48)
